import numpy as np
import ml_dtypes


def mxq(x, axis, fmt="e4m3"):
    dtype, down = {"e4m3": (ml_dtypes.float8_e4m3fn, 7), "e5m2": (ml_dtypes.float8_e5m2, 14)}[fmt]
    v = np.moveaxis(np.asarray(x, np.float32).astype(ml_dtypes.bfloat16).astype(np.float64), axis, -1)
    blocks = v.reshape(v.shape[:-1] + (-1, 32))
    amax = np.abs(blocks).max(-1, keepdims=True)
    byte = np.maximum(np.where(amax > 0, np.frexp(amax)[1] - 1 + 127, 0) - down, 1)
    scale = np.exp2(byte - 127.0)
    codes = (blocks / scale).astype(np.float32).astype(dtype).astype(np.float64)
    return np.moveaxis((codes * scale).reshape(v.shape), -1, axis)


WIDE = False


def mx_kscale(k):
    if not WIDE:
        return np.ones(k)
    levels = np.array([10, -10, 5, -5, 0])
    if k % 512:
        return np.exp2(np.random.permutation(np.resize(levels, k // 32))).repeat(32)
    a = np.empty((k // 512, 16))
    for p in range(k // 512):
        a[p, :8] = np.random.permutation(np.resize(levels, 8))
        for g in range(8):
            far = levels[np.abs(levels - a[p, g]) >= 10]
            a[p, g + 8] = far[np.random.randint(len(far))]
    return np.exp2(a.ravel()).repeat(32)


def f64(x):
    return np.asarray(x).astype(np.float64)


def striped(idx):
    return np.tile(idx.reshape(-1, 16).T, (8, 1)).astype(np.uint16)


def unstriped(offs):
    return offs[:16].T.reshape(-1).astype(np.int64)


def relu(v):
    return np.maximum(v, 0.0)


K, T, S, N = 512, 4096, 1024, 128
P = 2 ** 7


def setup_inputs():
    n = np.random.standard_normal
    s = mx_kscale(K)[:, None]
    return {
        "xT": (n((K, T)) * s).astype(np.float32),
        "tscale": np.tile(np.random.uniform(0.25, 2.0, T), (P, 1)).astype(np.float32),
        "cscale": np.random.uniform(0.5, 1.5, (N, 1)).astype(np.float32),
        "w1": (n((K, N)) / np.sqrt(K) / s).astype(np.float32),
        "offs": striped(np.random.permutation(T)[:S]),
    }


def reference(xT, tscale, cscale, w1, offs):
    xq = mxq(f64(xT)[:, unstriped(offs)], 0, "e4m3")
    y = mxq(f64(w1), 0, "e4m3").T @ xq
    tg = f64(tscale)[:1][:, unstriped(offs)]
    return relu((f64(cscale) * y) * tg)

@@ -1,0 +1,120 @@
+from contextlib import ExitStack
+
+import concourse.mybir as mybir
+from concourse.masks import make_identity
+
+K, T, S, N = 512, 4096, 1024, 128
+FLOPS = 2 * K * S * N
+BYTES = 4 * (K * T + T + N + K * N + N * S) + 2 * 128 * (S // 16)
+
+F32 = mybir.dt.float32
+BF16 = mybir.dt.bfloat16
+U32 = mybir.dt.uint32
+U16 = mybir.dt.uint16
+U8 = mybir.dt.uint8
+FP8X4 = mybir.dt.float8_e4m3fn_x4
+COPY = mybir.ActivationFunctionType.Copy
+RELU = mybir.ActivationFunctionType.Relu
+MULT = mybir.AluOpType.mult
+
+P = 128
+PACK = 4
+HALF = S // 2
+CHUNK = 256
+LAST_CUTS = [0,1024,2048,3072,3712,4096]
+VECTOR_CASTS = [2,3]
+
+
+def tile_picked_tokscale_relu_l_kernel(tc, xT, tscale, cscale, w1, offs, out):
+    nc = tc.nc
+    with ExitStack() as ctx:
+        keep = ctx.enter_context(tc.tile_pool(name="keep", bufs=1))
+        spread = ctx.enter_context(tc.psum_pool(name="spread", bufs=4))
+        accs = ctx.enter_context(tc.psum_pool(name="accs", bufs=1))
+
+        x_rows = xT.rearrange("(p j) t -> p j t", j=PACK)
+        planes = [keep.tile([P, T], F32, name="plane%d" % j) for j in range(PACK)]
+        offsets = keep.tile([P, S // 16], U16, name="offsets")
+        t_row = keep.tile([P, T // P], F32, name="t_row")
+        w_raw = keep.tile([P, PACK, N], F32, name="w_raw")
+        c_col = keep.tile([P, 1], F32, name="c_col")
+
+        nc.sync.dma_start(out=planes[0][:], in_=x_rows[:, 0, :])
+        nc.sync.dma_start(offsets[:], offs)
+        nc.scalar.dma_start(out=t_row[:], in_=tscale[0:1, :].rearrange("o (p m) -> (o p) m", p=P))
+        nc.scalar.dma_start(out=w_raw[:], in_=w1.rearrange("(p j) n -> p j n", j=PACK))
+        nc.scalar.dma_start(out=c_col[:], in_=cscale)
+        for j in (1, 2):
+            nc.sync.dma_start(out=planes[j][:], in_=x_rows[:, j, :])
+        for a, b in zip(LAST_CUTS[:-1], LAST_CUTS[1:]):
+            nc.sync.dma_start(out=planes[3][:, a:b], in_=x_rows[:, 3, a:b])
+
+        ident = keep.tile([P, P], F32, name="ident")
+        make_identity(nc, ident[:])
+
+        t_window = keep.tile([P, T], F32, name="t_window")
+        t_cols = t_window[:].rearrange("q (n m) -> q n m", m=T // P)
+        for b in range(T // P // 4):
+            bank = spread.tile([P, 4, P], F32, name="bank")
+            for i in range(4):
+                m = 4 * b + i
+                nc.tensor.transpose(bank[:, i, :], t_row[:, m : m + 1].to_broadcast([P, P]), ident[:])
+            nc.scalar.activation(t_cols[:, :, 4 * b : 4 * b + 4], bank[:].rearrange("q i n -> q n i"), COPY)
+
+        w_grouped = keep.tile([P, N, PACK], BF16, name="w_grouped", align_bytes=64)
+        nc.vector.tensor_copy(out=w_grouped[:], in_=w_raw[:].rearrange("p j n -> p n j"))
+        w_codes = keep.tile([P, N], U32, name="w_codes", align_bytes=64)
+        w_scales = keep.tile([P, N], U8, name="w_scales", align_bytes=64)
+        nc.vector.quantize_mx(out=w_codes[:].bitcast(FP8X4), scales=w_scales[:], in_=w_grouped[:].rearrange("p n j -> p (n j)"))
+
+        grouped = [keep.tile([P, HALF, PACK], BF16, name="grouped%d" % h, align_bytes=64) for h in range(2)]
+        half_offsets = [offsets[:, h * (HALF // 16) : (h + 1) * (HALF // 16)] for h in range(2)]
+        t_picked = keep.tile([P, S], F32, name="t_picked")
+
+        def gather(j, h):
+            nc.vector.tensor_copy(grouped[h][:, :, j], planes[j][:].indirect(half_offsets[h]))
+
+        for h in range(2):
+            gather(0, h)
+        nc.vector.tensor_copy(t_picked[:], t_window[:].indirect(offsets[:]))
+        for j in (1, 2):
+            for h in range(2):
+                gather(j, h)
+
+        last_bf16 = keep.tile([P, T], BF16, name="last_bf16")
+        for i, (a, b) in enumerate(zip(LAST_CUTS[:-1], LAST_CUTS[1:])):
+            if i not in VECTOR_CASTS:
+                nc.scalar.copy(last_bf16[:, a:b], planes[3][:, a:b])
+            else:
+                nc.vector.tensor_copy(last_bf16[:, a:b], planes[3][:, a:b])
+        gather(3, 0)
+        nc.scalar.activation(grouped[1][:, :, 3], last_bf16[:].indirect(half_offsets[1]), COPY)
+
+        banks = []
+        for c in range(S // CHUNK):
+            h, c0 = divmod(c * CHUNK, HALF)
+            codes = keep.tile([P, CHUNK], U32, name="codes%d" % c, align_bytes=64)
+            scales = keep.tile([P, CHUNK], U8, name="scales%d" % c, align_bytes=64)
+            nc.vector.quantize_mx(
+                out=codes[:].bitcast(FP8X4),
+                scales=scales[:],
+                in_=grouped[h][:, c0 : c0 + CHUNK, :].rearrange("p n j -> p (n j)"),
+            )
+            acc = accs.tile([P, CHUNK], F32, name="acc%d" % c)
+            nc.tensor.matmul_mx(
+                out=acc[:],
+                lhsT=w_codes[:].bitcast(FP8X4),
+                lhsT_scale=w_scales[:],
+                rhs=codes[:].bitcast(FP8X4),
+                rhs_scale=scales[:],
+                start=True,
+                stop=True,
+            )
+            banks.append(acc)
+        for c in range(S // CHUNK):
+            cols = slice(c * CHUNK, (c + 1) * CHUNK)
+            scaled = keep.tile([P, CHUNK], F32, name="scaled%d" % c)
+            nc.vector.tensor_tensor(scaled[:], banks[c][:], t_picked[:, cols], MULT)
+            result = keep.tile([P, CHUNK], F32, name="result%d" % c)
+            nc.scalar.activation(result[:], scaled[:], RELU, scale=c_col[:])
+            nc.sync.dma_start(out=out[:, cols], in_=result[:])

@@ -20,8 +20,8 @@ MULT = mybir.AluOpType.mult
 P = 128
 PACK = 4
 HALF = S // 2
-CHUNK = 256
-LAST_CUTS = [0,1024,2048,3072,3712,4096]
+CHUNK_CUTS = [0,256,512,768,896,1024]
+LAST_CUTS = [0,768,2048,3072,3584,4096]
 VECTOR_CASTS = [2,3]
 
 
@@ -29,30 +29,32 @@ def tile_picked_tokscale_relu_l_kernel(tc, xT, tscale, cscale, w1, offs, out):
     nc = tc.nc
     with ExitStack() as ctx:
         keep = ctx.enter_context(tc.tile_pool(name="keep", bufs=1))
-        spread = ctx.enter_context(tc.psum_pool(name="spread", bufs=4))
+        shared = ctx.enter_context(tc.tile_pool(name="shared", bufs=1))
+        spread = ctx.enter_context(tc.psum_pool(name="spread", bufs=3))
         accs = ctx.enter_context(tc.psum_pool(name="accs", bufs=1))
 
         x_rows = xT.rearrange("(p j) t -> p j t", j=PACK)
-        planes = [keep.tile([P, T], F32, name="plane%d" % j) for j in range(PACK)]
+        planes = [keep.tile([P, T], F32, name="plane%d" % j) for j in range(PACK - 1)]
+        planes.append(shared.tile([P, T], F32, name="plane3", offset=16384, align_bytes=64))
         offsets = keep.tile([P, S // 16], U16, name="offsets")
         t_row = keep.tile([P, T // P], F32, name="t_row")
-        w_raw = keep.tile([P, PACK, N], F32, name="w_raw")
+        w_raw = shared.tile([P, PACK, N], F32, name="w_raw", offset=32768, align_bytes=64)
         c_col = keep.tile([P, 1], F32, name="c_col")
 
+        nc.sync.dma_start(out=t_row[:], in_=tscale[0:1, :].rearrange("o (p m) -> (o p) m", p=P))
         nc.sync.dma_start(out=planes[0][:], in_=x_rows[:, 0, :])
         nc.sync.dma_start(offsets[:], offs)
-        nc.scalar.dma_start(out=t_row[:], in_=tscale[0:1, :].rearrange("o (p m) -> (o p) m", p=P))
-        nc.scalar.dma_start(out=w_raw[:], in_=w1.rearrange("(p j) n -> p j n", j=PACK))
         nc.scalar.dma_start(out=c_col[:], in_=cscale)
         for j in (1, 2):
             nc.sync.dma_start(out=planes[j][:], in_=x_rows[:, j, :])
         for a, b in zip(LAST_CUTS[:-1], LAST_CUTS[1:]):
             nc.sync.dma_start(out=planes[3][:, a:b], in_=x_rows[:, 3, a:b])
+        nc.sync.dma_start(out=w_raw[:], in_=w1.rearrange("(p j) n -> p j n", j=PACK))
 
         ident = keep.tile([P, P], F32, name="ident")
         make_identity(nc, ident[:])
 
-        t_window = keep.tile([P, T], F32, name="t_window")
+        t_window = shared.tile([P, T], F32, name="t_window", offset=0, align_bytes=64)
         t_cols = t_window[:].rearrange("q (n m) -> q n m", m=T // P)
         for b in range(T // P // 4):
             bank = spread.tile([P, 4, P], F32, name="bank")
@@ -61,27 +63,24 @@ def tile_picked_tokscale_relu_l_kernel(tc, xT, tscale, cscale, w1, offs, out):
                 nc.tensor.transpose(bank[:, i, :], t_row[:, m : m + 1].to_broadcast([P, P]), ident[:])
             nc.scalar.activation(t_cols[:, :, 4 * b : 4 * b + 4], bank[:].rearrange("q i n -> q n i"), COPY)
 
-        w_grouped = keep.tile([P, N, PACK], BF16, name="w_grouped", align_bytes=64)
-        nc.vector.tensor_copy(out=w_grouped[:], in_=w_raw[:].rearrange("p j n -> p n j"))
-        w_codes = keep.tile([P, N], U32, name="w_codes", align_bytes=64)
-        w_scales = keep.tile([P, N], U8, name="w_scales", align_bytes=64)
-        nc.vector.quantize_mx(out=w_codes[:].bitcast(FP8X4), scales=w_scales[:], in_=w_grouped[:].rearrange("p n j -> p (n j)"))
-
-        grouped = [keep.tile([P, HALF, PACK], BF16, name="grouped%d" % h, align_bytes=64) for h in range(2)]
+        grouped = [shared.tile([P, HALF, PACK], BF16, name="grouped%d" % h, offset=4096 * h, align_bytes=64) for h in range(2)]
         half_offsets = [offsets[:, h * (HALF // 16) : (h + 1) * (HALF // 16)] for h in range(2)]
         t_picked = keep.tile([P, S], F32, name="t_picked")
+        last_bf16 = shared.tile([P, T], BF16, name="last_bf16", offset=8192, align_bytes=64)
+        blocks = last_bf16[:].rearrange("p (b n) -> p b n", n=HALF)
+        early = [blocks[:, 1:8:6, :], blocks[:, 2:4, :]]
 
         def gather(j, h):
             nc.vector.tensor_copy(grouped[h][:, :, j], planes[j][:].indirect(half_offsets[h]))
 
-        for h in range(2):
-            gather(0, h)
         nc.vector.tensor_copy(t_picked[:], t_window[:].indirect(offsets[:]))
-        for j in (1, 2):
-            for h in range(2):
-                gather(j, h)
+        for h in (1, 0):
+            for j in range(2):
+                nc.vector.tensor_copy(early[h][:, j, :], planes[j][:].indirect(half_offsets[h]))
+            nc.scalar.copy(grouped[h][:, :, 0:2], early[h].rearrange("p j n -> p n j"))
+        for h in (1, 0):
+            gather(2, h)
 
-        last_bf16 = keep.tile([P, T], BF16, name="last_bf16")
         for i, (a, b) in enumerate(zip(LAST_CUTS[:-1], LAST_CUTS[1:])):
             if i not in VECTOR_CASTS:
                 nc.scalar.copy(last_bf16[:, a:b], planes[3][:, a:b])
@@ -90,17 +89,32 @@ def tile_picked_tokscale_relu_l_kernel(tc, xT, tscale, cscale, w1, offs, out):
         gather(3, 0)
         nc.scalar.activation(grouped[1][:, :, 3], last_bf16[:].indirect(half_offsets[1]), COPY)
 
-        banks = []
-        for c in range(S // CHUNK):
-            h, c0 = divmod(c * CHUNK, HALF)
-            codes = keep.tile([P, CHUNK], U32, name="codes%d" % c, align_bytes=64)
-            scales = keep.tile([P, CHUNK], U8, name="scales%d" % c, align_bytes=64)
+        w_grouped = shared.tile([P, N, PACK], BF16, name="w_grouped", offset=16384, align_bytes=64)
+        nc.vector.tensor_copy(out=w_grouped[:], in_=w_raw[:].rearrange("p j n -> p n j"))
+        w_codes = keep.tile([P, N], U32, name="w_codes", align_bytes=64)
+        w_scales = keep.tile([P, N], U8, name="w_scales", align_bytes=64)
+
+        chunks = list(zip(CHUNK_CUTS[:-1], CHUNK_CUTS[1:]))
+        operands = []
+        for c, (a, b) in enumerate(chunks):
+            h, c0 = divmod(a, HALF)
+            if h == 0:
+                codes = shared.tile([P, b - a], U32, name="codes%d" % c, offset=32768 + 4 * a, align_bytes=64)
+            else:
+                codes = keep.tile([P, b - a], U32, name="codes%d" % c, align_bytes=64)
+            scales = keep.tile([P, b - a], U8, name="scales%d" % c, align_bytes=64)
             nc.vector.quantize_mx(
                 out=codes[:].bitcast(FP8X4),
                 scales=scales[:],
-                in_=grouped[h][:, c0 : c0 + CHUNK, :].rearrange("p n j -> p (n j)"),
+                in_=grouped[h][:, c0 : c0 + b - a, :].rearrange("p n j -> p (n j)"),
             )
-            acc = accs.tile([P, CHUNK], F32, name="acc%d" % c)
+            if c == 0:
+                nc.vector.quantize_mx(out=w_codes[:].bitcast(FP8X4), scales=w_scales[:], in_=w_grouped[:].rearrange("p n j -> p (n j)"))
+            operands.append((codes, scales))
+        banks = []
+        for c, (a, b) in enumerate(chunks):
+            codes, scales = operands[c]
+            acc = accs.tile([P, b - a], F32, name="acc%d" % c)
             nc.tensor.matmul_mx(
                 out=acc[:],
                 lhsT=w_codes[:].bitcast(FP8X4),
@@ -111,10 +125,9 @@ def tile_picked_tokscale_relu_l_kernel(tc, xT, tscale, cscale, w1, offs, out):
                 stop=True,
             )
             banks.append(acc)
-        for c in range(S // CHUNK):
-            cols = slice(c * CHUNK, (c + 1) * CHUNK)
-            scaled = keep.tile([P, CHUNK], F32, name="scaled%d" % c)
-            nc.vector.tensor_tensor(scaled[:], banks[c][:], t_picked[:, cols], MULT)
-            result = keep.tile([P, CHUNK], F32, name="result%d" % c)
+        for c, (a, b) in enumerate(chunks):
+            scaled = keep.tile([P, b - a], F32, name="scaled%d" % c)
+            nc.vector.tensor_tensor(scaled[:], banks[c][:], t_picked[:, a:b], MULT)
+            result = keep.tile([P, b - a], F32, name="result%d" % c)
             nc.scalar.activation(result[:], scaled[:], RELU, scale=c_col[:])
-            nc.sync.dma_start(out=out[:, cols], in_=result[:])
+            nc.sync.dma_start(out=out[:, a:b], in_=result[:])

@@ -35,27 +35,29 @@ def tile_picked_tokscale_relu_l_kernel(tc, xT, tscale, cscale, w1, offs, out):
 
         x_rows = xT.rearrange("(p j) t -> p j t", j=PACK)
         planes = [keep.tile([P, T], F32, name="plane%d" % j) for j in range(PACK - 1)]
-        planes.append(shared.tile([P, T], F32, name="plane3", offset=16384, align_bytes=64))
+        planes.append(shared.tile([P, T], F32, name="plane3", offset=0, align_bytes=64))
         offsets = keep.tile([P, S // 16], U16, name="offsets")
         t_row = keep.tile([P, T // P], F32, name="t_row")
-        w_raw = shared.tile([P, PACK, N], F32, name="w_raw", offset=32768, align_bytes=64)
+        w_raw = shared.tile([P, PACK, N], F32, name="w_raw", offset=16384, align_bytes=64)
         c_col = keep.tile([P, 1], F32, name="c_col")
 
         nc.sync.dma_start(out=t_row[:], in_=tscale[0:1, :].rearrange("o (p m) -> (o p) m", p=P))
         nc.sync.dma_start(out=planes[0][:], in_=x_rows[:, 0, :])
         nc.sync.dma_start(offsets[:], offs)
-        nc.scalar.dma_start(out=c_col[:], in_=cscale)
         for j in (1, 2):
             nc.sync.dma_start(out=planes[j][:], in_=x_rows[:, j, :])
         for a, b in zip(LAST_CUTS[:-1], LAST_CUTS[1:]):
             nc.sync.dma_start(out=planes[3][:, a:b], in_=x_rows[:, 3, a:b])
         nc.sync.dma_start(out=w_raw[:], in_=w1.rearrange("(p j) n -> p j n", j=PACK))
+        nc.sync.dma_start(out=c_col[:], in_=cscale)
 
         ident = keep.tile([P, P], F32, name="ident")
         make_identity(nc, ident[:])
 
-        t_window = shared.tile([P, T], F32, name="t_window", offset=0, align_bytes=64)
-        t_cols = t_window[:].rearrange("q (n m) -> q n m", m=T // P)
+        stage = keep.tile([P, HALF + T], F32, name="stage", align_bytes=64)
+        t_window = stage[:, HALF:]
+        stage_bf16 = stage[:].bitcast(BF16)
+        t_cols = t_window.rearrange("q (n m) -> q n m", m=T // P)
         for b in range(T // P // 4):
             bank = spread.tile([P, 4, P], F32, name="bank")
             for i in range(4):
@@ -63,20 +65,21 @@ def tile_picked_tokscale_relu_l_kernel(tc, xT, tscale, cscale, w1, offs, out):
                 nc.tensor.transpose(bank[:, i, :], t_row[:, m : m + 1].to_broadcast([P, P]), ident[:])
             nc.scalar.activation(t_cols[:, :, 4 * b : 4 * b + 4], bank[:].rearrange("q i n -> q n i"), COPY)
 
-        grouped = [shared.tile([P, HALF, PACK], BF16, name="grouped%d" % h, offset=4096 * h, align_bytes=64) for h in range(2)]
+        grouped = [stage_bf16[:, T + h * HALF * PACK : T + (h + 1) * HALF * PACK].rearrange("p (n j) -> p n j", j=PACK) for h in range(2)]
         half_offsets = [offsets[:, h * (HALF // 16) : (h + 1) * (HALF // 16)] for h in range(2)]
         t_picked = keep.tile([P, S], F32, name="t_picked")
-        last_bf16 = shared.tile([P, T], BF16, name="last_bf16", offset=8192, align_bytes=64)
-        blocks = last_bf16[:].rearrange("p (b n) -> p b n", n=HALF)
-        early = [blocks[:, 1:8:6, :], blocks[:, 2:4, :]]
+        last_bf16 = stage_bf16[:, 0:T]
+        blocks = last_bf16.rearrange("p (b n) -> p b n", n=HALF)
+        early = [blocks[:, 1:8:6, :], blocks[:, 0:3:2, :]]
 
         def gather(j, h):
             nc.vector.tensor_copy(grouped[h][:, :, j], planes[j][:].indirect(half_offsets[h]))
 
-        nc.vector.tensor_copy(t_picked[:], t_window[:].indirect(offsets[:]))
         for h in (1, 0):
-            for j in range(2):
-                nc.vector.tensor_copy(early[h][:, j, :], planes[j][:].indirect(half_offsets[h]))
+            nc.vector.tensor_copy(early[h][:, 0, :], planes[0][:].indirect(half_offsets[h]))
+        nc.vector.tensor_copy(t_picked[:], t_window.indirect(offsets[:]))
+        for h in (1, 0):
+            nc.vector.tensor_copy(early[h][:, 1, :], planes[1][:].indirect(half_offsets[h]))
             nc.scalar.copy(grouped[h][:, :, 0:2], early[h].rearrange("p j n -> p n j"))
         for h in (1, 0):
             gather(2, h)
@@ -87,9 +90,9 @@ def tile_picked_tokscale_relu_l_kernel(tc, xT, tscale, cscale, w1, offs, out):
             else:
                 nc.vector.tensor_copy(last_bf16[:, a:b], planes[3][:, a:b])
         gather(3, 0)
-        nc.scalar.activation(grouped[1][:, :, 3], last_bf16[:].indirect(half_offsets[1]), COPY)
+        nc.scalar.activation(grouped[1][:, :, 3], last_bf16.indirect(half_offsets[1]), COPY)
 
-        w_grouped = shared.tile([P, N, PACK], BF16, name="w_grouped", offset=16384, align_bytes=64)
+        w_grouped = shared.tile([P, N, PACK], BF16, name="w_grouped", offset=0, align_bytes=64)
         nc.vector.tensor_copy(out=w_grouped[:], in_=w_raw[:].rearrange("p j n -> p n j"))
         w_codes = keep.tile([P, N], U32, name="w_codes", align_bytes=64)
         w_scales = keep.tile([P, N], U8, name="w_scales", align_bytes=64)
@@ -99,7 +102,7 @@ def tile_picked_tokscale_relu_l_kernel(tc, xT, tscale, cscale, w1, offs, out):
         for c, (a, b) in enumerate(chunks):
             h, c0 = divmod(a, HALF)
             if h == 0:
-                codes = shared.tile([P, b - a], U32, name="codes%d" % c, offset=32768 + 4 * a, align_bytes=64)
+                codes = shared.tile([P, b - a], U32, name="codes%d" % c, offset=16384 + 4 * a, align_bytes=64)
             else:
                 codes = keep.tile([P, b - a], U32, name="codes%d" % c, align_bytes=64)
             scales = keep.tile([P, b - a], U8, name="scales%d" % c, align_bytes=64)

@@ -38,7 +38,7 @@ def tile_picked_tokscale_relu_l_kernel(tc, xT, tscale, cscale, w1, offs, out):
         planes.append(shared.tile([P, T], F32, name="plane3", offset=0, align_bytes=64))
         offsets = keep.tile([P, S // 16], U16, name="offsets")
         t_row = keep.tile([P, T // P], F32, name="t_row")
-        w_raw = shared.tile([P, PACK, N], F32, name="w_raw", offset=16384, align_bytes=64)
+        w_raw = keep.tile([P, PACK, N], F32, name="w_raw")
         c_col = keep.tile([P, 1], F32, name="c_col")
 
         nc.sync.dma_start(out=t_row[:], in_=tscale[0:1, :].rearrange("o (p m) -> (o p) m", p=P))
@@ -92,17 +92,18 @@ def tile_picked_tokscale_relu_l_kernel(tc, xT, tscale, cscale, w1, offs, out):
         gather(3, 0)
         nc.scalar.activation(grouped[1][:, :, 3], last_bf16.indirect(half_offsets[1]), COPY)
 
-        w_grouped = shared.tile([P, N, PACK], BF16, name="w_grouped", offset=0, align_bytes=64)
-        nc.vector.tensor_copy(out=w_grouped[:], in_=w_raw[:].rearrange("p j n -> p n j"))
-        w_codes = keep.tile([P, N], U32, name="w_codes", align_bytes=64)
+        w_grouped = keep.tile([P, N, PACK], BF16, name="w_grouped", align_bytes=64)
+        nc.gpsimd.tensor_scalar(w_grouped[:], w_raw[:].rearrange("p j n -> p n j"), 1.0, 0.0, MULT, mybir.AluOpType.add)
+        w_codes = shared.tile([P, N], U32, name="w_codes", offset=4 * HALF, align_bytes=64)
         w_scales = keep.tile([P, N], U8, name="w_scales", align_bytes=64)
+        nc.vector.quantize_mx(out=w_codes[:].bitcast(FP8X4), scales=w_scales[:], in_=w_grouped[:].rearrange("p n j -> p (n j)"))
 
         chunks = list(zip(CHUNK_CUTS[:-1], CHUNK_CUTS[1:]))
         operands = []
         for c, (a, b) in enumerate(chunks):
             h, c0 = divmod(a, HALF)
             if h == 0:
-                codes = shared.tile([P, b - a], U32, name="codes%d" % c, offset=16384 + 4 * a, align_bytes=64)
+                codes = shared.tile([P, b - a], U32, name="codes%d" % c, offset=4 * a, align_bytes=64)
             else:
                 codes = keep.tile([P, b - a], U32, name="codes%d" % c, align_bytes=64)
             scales = keep.tile([P, b - a], U8, name="scales%d" % c, align_bytes=64)
@@ -111,8 +112,6 @@ def tile_picked_tokscale_relu_l_kernel(tc, xT, tscale, cscale, w1, offs, out):
                 scales=scales[:],
                 in_=grouped[h][:, c0 : c0 + b - a, :].rearrange("p n j -> p (n j)"),
             )
-            if c == 0:
-                nc.vector.quantize_mx(out=w_codes[:].bitcast(FP8X4), scales=w_scales[:], in_=w_grouped[:].rearrange("p n j -> p (n j)"))
             operands.append((codes, scales))
         banks = []
         for c, (a, b) in enumerate(chunks):

from contextlib import ExitStack

import concourse.mybir as mybir
from concourse.masks import make_identity

K, T, S, N = 512, 4096, 1024, 128
FLOPS = 2 * K * S * N
BYTES = 4 * (K * T + T + N + K * N + N * S) + 2 * 128 * (S // 16)

F32 = mybir.dt.float32
BF16 = mybir.dt.bfloat16
U32 = mybir.dt.uint32
U16 = mybir.dt.uint16
U8 = mybir.dt.uint8
FP8X4 = mybir.dt.float8_e4m3fn_x4
COPY = mybir.ActivationFunctionType.Copy
RELU = mybir.ActivationFunctionType.Relu
MULT = mybir.AluOpType.mult

P = 128
PACK = 4
HALF = S // 2
CHUNK_CUTS = [0,256,512,768,896,1024]
LAST_CUTS = [0,768,2048,3072,3584,4096]
VECTOR_CASTS = [2,3]


def tile_picked_tokscale_relu_l_kernel(tc, xT, tscale, cscale, w1, offs, out):
    nc = tc.nc
    with ExitStack() as ctx:
        keep = ctx.enter_context(tc.tile_pool(name="keep", bufs=1))
        shared = ctx.enter_context(tc.tile_pool(name="shared", bufs=1))
        spread = ctx.enter_context(tc.psum_pool(name="spread", bufs=3))
        accs = ctx.enter_context(tc.psum_pool(name="accs", bufs=1))

        x_rows = xT.rearrange("(p j) t -> p j t", j=PACK)
        planes = [keep.tile([P, T], F32, name="plane%d" % j) for j in range(PACK - 1)]
        planes.append(shared.tile([P, T], F32, name="plane3", offset=0, align_bytes=64))
        offsets = keep.tile([P, S // 16], U16, name="offsets")
        t_row = keep.tile([P, T // P], F32, name="t_row")
        w_raw = keep.tile([P, PACK, N], F32, name="w_raw")
        c_col = keep.tile([P, 1], F32, name="c_col")

        nc.sync.dma_start(out=t_row[:], in_=tscale[0:1, :].rearrange("o (p m) -> (o p) m", p=P))
        nc.sync.dma_start(out=planes[0][:], in_=x_rows[:, 0, :])
        nc.sync.dma_start(offsets[:], offs)
        for j in (1, 2):
            nc.sync.dma_start(out=planes[j][:], in_=x_rows[:, j, :])
        for a, b in zip(LAST_CUTS[:-1], LAST_CUTS[1:]):
            nc.sync.dma_start(out=planes[3][:, a:b], in_=x_rows[:, 3, a:b])
        nc.sync.dma_start(out=w_raw[:], in_=w1.rearrange("(p j) n -> p j n", j=PACK))
        nc.sync.dma_start(out=c_col[:], in_=cscale)

        ident = keep.tile([P, P], F32, name="ident")
        make_identity(nc, ident[:])

        stage = keep.tile([P, HALF + T], F32, name="stage", align_bytes=64)
        t_window = stage[:, HALF:]
        stage_bf16 = stage[:].bitcast(BF16)
        t_cols = t_window.rearrange("q (n m) -> q n m", m=T // P)
        for b in range(T // P // 4):
            bank = spread.tile([P, 4, P], F32, name="bank")
            for i in range(4):
                m = 4 * b + i
                nc.tensor.transpose(bank[:, i, :], t_row[:, m : m + 1].to_broadcast([P, P]), ident[:])
            nc.scalar.activation(t_cols[:, :, 4 * b : 4 * b + 4], bank[:].rearrange("q i n -> q n i"), COPY)

        grouped = [stage_bf16[:, T + h * HALF * PACK : T + (h + 1) * HALF * PACK].rearrange("p (n j) -> p n j", j=PACK) for h in range(2)]
        half_offsets = [offsets[:, h * (HALF // 16) : (h + 1) * (HALF // 16)] for h in range(2)]
        t_picked = keep.tile([P, S], F32, name="t_picked")
        last_bf16 = stage_bf16[:, 0:T]
        blocks = last_bf16.rearrange("p (b n) -> p b n", n=HALF)
        early = [blocks[:, 1:8:6, :], blocks[:, 0:3:2, :]]

        def gather(j, h):
            nc.vector.tensor_copy(grouped[h][:, :, j], planes[j][:].indirect(half_offsets[h]))

        for h in (1, 0):
            nc.vector.tensor_copy(early[h][:, 0, :], planes[0][:].indirect(half_offsets[h]))
        nc.vector.tensor_copy(t_picked[:], t_window.indirect(offsets[:]))
        for h in (1, 0):
            nc.vector.tensor_copy(early[h][:, 1, :], planes[1][:].indirect(half_offsets[h]))
            nc.scalar.copy(grouped[h][:, :, 0:2], early[h].rearrange("p j n -> p n j"))
        for h in (1, 0):
            gather(2, h)

        for i, (a, b) in enumerate(zip(LAST_CUTS[:-1], LAST_CUTS[1:])):
            if i not in VECTOR_CASTS:
                nc.scalar.copy(last_bf16[:, a:b], planes[3][:, a:b])
            else:
                nc.vector.tensor_copy(last_bf16[:, a:b], planes[3][:, a:b])
        gather(3, 0)
        nc.scalar.activation(grouped[1][:, :, 3], last_bf16.indirect(half_offsets[1]), COPY)

        w_grouped = keep.tile([P, N, PACK], BF16, name="w_grouped", align_bytes=64)
        nc.gpsimd.tensor_scalar(w_grouped[:], w_raw[:].rearrange("p j n -> p n j"), 1.0, 0.0, MULT, mybir.AluOpType.add)
        w_codes = shared.tile([P, N], U32, name="w_codes", offset=4 * HALF, align_bytes=64)
        w_scales = keep.tile([P, N], U8, name="w_scales", align_bytes=64)
        nc.vector.quantize_mx(out=w_codes[:].bitcast(FP8X4), scales=w_scales[:], in_=w_grouped[:].rearrange("p n j -> p (n j)"))

        chunks = list(zip(CHUNK_CUTS[:-1], CHUNK_CUTS[1:]))
        operands = []
        for c, (a, b) in enumerate(chunks):
            h, c0 = divmod(a, HALF)
            if h == 0:
                codes = shared.tile([P, b - a], U32, name="codes%d" % c, offset=4 * a, align_bytes=64)
            else:
                codes = keep.tile([P, b - a], U32, name="codes%d" % c, align_bytes=64)
            scales = keep.tile([P, b - a], U8, name="scales%d" % c, align_bytes=64)
            nc.vector.quantize_mx(
                out=codes[:].bitcast(FP8X4),
                scales=scales[:],
                in_=grouped[h][:, c0 : c0 + b - a, :].rearrange("p n j -> p (n j)"),
            )
            operands.append((codes, scales))
        banks = []
        for c, (a, b) in enumerate(chunks):
            codes, scales = operands[c]
            acc = accs.tile([P, b - a], F32, name="acc%d" % c)
            nc.tensor.matmul_mx(
                out=acc[:],
                lhsT=w_codes[:].bitcast(FP8X4),
                lhsT_scale=w_scales[:],
                rhs=codes[:].bitcast(FP8X4),
                rhs_scale=scales[:],
                start=True,
                stop=True,
            )
            banks.append(acc)
        for c, (a, b) in enumerate(chunks):
            scaled = keep.tile([P, b - a], F32, name="scaled%d" % c)
            nc.vector.tensor_tensor(scaled[:], banks[c][:], t_picked[:, a:b], MULT)
            result = keep.tile([P, b - a], F32, name="result%d" % c)
            nc.scalar.activation(result[:], scaled[:], RELU, scale=c_col[:])
            nc.sync.dma_start(out=out[:, a:b], in_=result[:])
